import numpy as np
import ml_dtypes


def mxq(x, axis, fmt="e4m3"):
    dtype, down = {"e4m3": (ml_dtypes.float8_e4m3fn, 7), "e5m2": (ml_dtypes.float8_e5m2, 14)}[fmt]
    v = np.moveaxis(np.asarray(x, np.float32).astype(ml_dtypes.bfloat16).astype(np.float64), axis, -1)
    blocks = v.reshape(v.shape[:-1] + (-1, 32))
    amax = np.abs(blocks).max(-1, keepdims=True)
    byte = np.maximum(np.where(amax > 0, np.frexp(amax)[1] - 1 + 127, 0) - down, 1)
    scale = np.exp2(byte - 127.0)
    codes = (blocks / scale).astype(np.float32).astype(dtype).astype(np.float64)
    return np.moveaxis((codes * scale).reshape(v.shape), -1, axis)


WIDE = False


def mx_kscale(k):
    if not WIDE:
        return np.ones(k)
    levels = np.array([10, -10, 5, -5, 0])
    if k % 512:
        return np.exp2(np.random.permutation(np.resize(levels, k // 32))).repeat(32)
    a = np.empty((k // 512, 16))
    for p in range(k // 512):
        a[p, :8] = np.random.permutation(np.resize(levels, 8))
        for g in range(8):
            far = levels[np.abs(levels - a[p, g]) >= 10]
            a[p, g + 8] = far[np.random.randint(len(far))]
    return np.exp2(a.ravel()).repeat(32)


def f64(x):
    return np.asarray(x).astype(np.float64)


def striped(idx):
    return np.tile(idx.reshape(-1, 16).T, (8, 1)).astype(np.uint16)


def unstriped(offs):
    return offs[:16].T.reshape(-1).astype(np.int64)


def pack_weight(w):
    k, n = w.shape
    w = f64(np.asarray(w, np.float32).astype(ml_dtypes.bfloat16)).reshape(k // 32, 32, n)
    amax = np.abs(w).max(1)
    byte = np.clip(np.where(amax > 0, np.frexp(amax)[1] - 1 + 127 - 7, 1), 1, 254)
    scaled = (w * np.exp2(127.0 - byte)[:, None, :]).reshape(k, n).astype(np.float32)
    words = np.ascontiguousarray(scaled.reshape(k // 512, 128, 4, n).transpose(0, 1, 3, 2)).astype(ml_dtypes.float8_e4m3fn).view(np.uint8)
    return words, np.ascontiguousarray(byte.astype(np.uint8).reshape(k // 512, 16, n))


def unpack_weight(words, scales):
    g, p, n, _ = words.shape
    vals = np.ascontiguousarray(words).view(ml_dtypes.float8_e4m3fn).astype(np.float64) * np.repeat(np.exp2(scales.astype(np.float64) - 127.0), 8, axis=1)[..., None]
    return vals.transpose(0, 1, 3, 2).reshape(g * 512, n)


K, T, S, D, N, H, V, U = 1024, 4096, 1024, 4, 128, 512, 256, 512


def setup_inputs():
    n = np.random.standard_normal
    s = mx_kscale(K)[:, None]
    u = mx_kscale(H)
    packed_xT = pack_weight(n((K, T)) * s)
    return {
        "x_words": packed_xT[0],
        "x_scales": packed_xT[1],
        "hT": (n((K, H)) / np.sqrt(K) / s).astype(np.float32),
        "unit": (np.random.uniform(0.6, 1.4, (H, 1)) * u[:, None]).astype(np.float32),
        "w1": (n((H, N)) / np.sqrt(H) / u[:, None]).astype(np.float32),
        "offs": striped(np.random.permutation(T)[:S]),
        "pos": striped(np.random.permutation(np.concatenate([np.arange(V), np.random.randint(0, V, U - V)]))),
        "neg": striped(np.random.permutation(np.concatenate([np.arange(V), np.random.randint(0, V, U - V)]))),
    }


def reference(x_words, x_scales, hT, unit, w1, offs, pos, neg):
    hTq = mxq(f64(hT), 0, "e4m3")
    xq = unpack_weight(x_words, x_scales)[:, unstriped(offs)]
    y = hTq.T @ xq
    ww = np.exp(1.5 * np.tanh(y))
    wy = ww * y
    bag = (wy.reshape(len(wy), -1, D).sum(axis=2)) / (ww.reshape(len(ww), -1, D).sum(axis=2))
    bp = bag[:, unstriped(pos)]
    bn = bag[:, unstriped(neg)]
    mar = bp - bn
    ls = np.log(np.exp(-1.0 * mar) + 1.0)
    top = y.reshape(len(y), -1, D).max(axis=2)
    tp = top[:, unstriped(pos)]
    hid = f64(unit) * (ls * tp)
    return mxq(f64(w1), 0, "e4m3").T @ mxq(hid, 0, "e4m3")

@@ -1,0 +1,331 @@
+import math
+from contextlib import ExitStack
+
+import concourse.mybir as mybir
+from concourse.masks import make_identity
+
+K, T, S, D, N, H, V, U = 1024, 4096, 1024, 4, 128, 512, 256, 512
+FLOPS = 2 * K * H * S + 2 * H * N * U
+
+F32 = mybir.dt.float32
+BF16 = mybir.dt.bfloat16
+I32 = mybir.dt.int32
+U32 = mybir.dt.uint32
+U16 = mybir.dt.uint16
+U8 = mybir.dt.uint8
+FP8X4 = mybir.dt.float8_e4m3fn_x4
+ACT = mybir.ActivationFunctionType
+ALU = mybir.AluOpType
+AXIS = mybir.AxisListType
+
+P = 128
+PACK = 4
+PASSES = K // (P * PACK)
+HALVES = V // P
+BLOCKS = H // P
+RUN = P // PACK
+KNEE = 32.0
+BAG_WINDOW = 1024
+TOP_WINDOW = 544
+H_LOADS = ((0, 1), (1, 2), (2, 4))
+UNITS = ((0, 0), (0, 1), (1, 0), (2, 0), (3, 0), (1, 1), (2, 1), (3, 1))
+PAIR_CHUNKS = ((0, 256), (256, 512))
+
+
+def tile_picked_ymilrk_top_p_kernel(
+    tc, x_words, x_scales, hT, unit, w1, offs, pos, neg, out
+):
+    nc = tc.nc
+    with ExitStack() as ctx:
+        keep = ctx.enter_context(tc.tile_pool(name="keep", bufs=1))
+        ring = ctx.enter_context(tc.tile_pool(name="ring", bufs=2))
+        y_psum = ctx.enter_context(tc.psum_pool(name="y_psum", bufs=3))
+        sum_psum = ctx.enter_context(tc.psum_pool(name="sum_psum", bufs=4))
+        top_psum = ctx.enter_context(tc.psum_pool(name="top_psum", bufs=1))
+
+        offs_t = keep.tile([P, S // 16], U16, name="offs_t")
+        pos_t = keep.tile([P, U // 16], U16, name="pos_t")
+        neg_t = keep.tile([P, U // 16], U16, name="neg_t")
+        x_table = [keep.tile([P, T], U32, name=f"x_table{o}") for o in range(PASSES)]
+        s_table = keep.tile([P, T], U8, name="s_table")
+        h_raw = {}
+        for first, last in H_LOADS:
+            for o in range(PASSES):
+                h_raw[first, o] = keep.tile([P, PACK, (last - first) * P], F32, name=f"h_raw{first}_{o}")
+        unit_raw = keep.tile([P, PACK], F32, name="unit_raw")
+        w_raw = keep.tile([P, PACK, N], F32, name="w_raw")
+
+        def load_words(o, a, b):
+            nc.sync.dma_start(
+                x_table[o][:, a:b].bitcast(I32), x_words[o, :, a:b].rearrange("p n t -> p (n t)").bitcast(I32)
+            )
+
+        def load_h(first, last):
+            for o in range(PASSES):
+                rows = hT[o * P * PACK : (o + 1) * P * PACK, first * P : last * P]
+                nc.sync.dma_start(h_raw[first, o][:], rows.rearrange("(p j) n -> p j n", j=PACK))
+
+        nc.vector.memset(s_table[:].bitcast(I32), 0)
+        load_words(0, 0, T // 2)
+        for q in range(4):
+            nc.sync.dma_start(
+                s_table[32 * q : 32 * q + 4 * PASSES, :].bitcast(I32),
+                x_scales[:, 4 * q : 4 * q + 4, :].bitcast(I32),
+            )
+        nc.sync.dma_start(offs_t[:], offs)
+        load_words(0, T // 2, T)
+        load_words(1, 0, T)
+        for first, last in H_LOADS:
+            load_h(first, last)
+        nc.sync.dma_start(unit_raw[:], unit.rearrange("(p t) one -> p (t one)", t=PACK))
+        nc.sync.dma_start(pos_t[:], pos)
+        nc.sync.dma_start(neg_t[:], neg)
+        nc.sync.dma_start(w_raw[:], w1.rearrange("(p j) m -> p j m", j=PACK))
+
+        ident = keep.tile([P, P], F32, name="ident")
+        make_identity(nc, ident[:])
+        bag = [keep.tile([P, BAG_WINDOW], F32, name=f"bag{t}") for t in range(PACK)]
+        top = [keep.tile([P, TOP_WINDOW], F32, name=f"top{t}") for t in range(PACK)]
+        for t in range(PACK):
+            nc.vector.memset(bag[t][:, V:], 0.0)
+            nc.vector.memset(top[t][:, V:], 0.0)
+
+        unit_knee = keep.tile([P, PACK], F32, name="unit_knee")
+        nc.scalar.mul(unit_knee[:], unit_raw[:], 1.0 / KNEE)
+
+        def interleave(engine, grouped, raw):
+            src = raw.rearrange("p j (c i) -> p c j i", i=4)
+            dst = grouped.rearrange("p (c i) j -> p c j i", i=4)
+            if engine == "scalar":
+                nc.scalar.copy(dst, src)
+            else:
+                nc.vector.tensor_copy(dst, src)
+
+        w_grouped = keep.tile([P, N, PACK], BF16, name="w_grouped", align_bytes=64)
+        w_codes = keep.tile([P, N], U32, name="w_codes", align_bytes=64)
+        w_scales = keep.tile([P, N], U8, name="w_scales", align_bytes=64)
+
+        s_picked = keep.tile([P, S], U8, name="s_picked")
+        s_dealt = keep.tile([P, HALVES, D, P], U8, name="s_dealt", align_bytes=64)
+        x_picked = {}
+
+        def pick_words(o, half):
+            x_picked[o, half] = keep.tile([P, D, P], U32, name=f"x_picked{o}_{half}", align_bytes=64)
+            cols = S // 16 // HALVES
+            nc.vector.tensor_copy(
+                x_picked[o, half][:].rearrange("p d v -> p v d"),
+                x_table[o][:].indirect(offs_t[:, half * cols : (half + 1) * cols]),
+            )
+
+        h_codes = {}
+        h_scales = {}
+
+        def quantize_h(c, engines):
+            first = max(f for f, last in H_LOADS if f <= c)
+            cols = slice((c - first) * P, (c - first + 1) * P)
+            grouped = keep.tile([P, PASSES, P, PACK], BF16, name=f"h_grouped{c}", align_bytes=64)
+            h_codes[c] = keep.tile([P, PASSES, P], U32, name=f"h_codes{c}", align_bytes=64)
+            h_scales[c] = keep.tile([P, PASSES, P], U8, name=f"h_scales{c}", align_bytes=64)
+            for o in range(PASSES):
+                interleave(engines[o], grouped[:, o], h_raw[first, o][:, :, cols])
+            nc.vector.quantize_mx(
+                h_codes[c][:].rearrange("p o n -> p (o n)").bitcast(FP8X4),
+                h_scales[c][:].rearrange("p o n -> p (o n)"),
+                grouped[:].rearrange("p o n j -> p (o n j)"),
+            )
+
+        ww = [keep.tile([P, D, PACK, BLOCKS, RUN], F32, name=f"ww{h}") for h in range(HALVES)]
+        wy = [keep.tile([P, D, PACK, BLOCKS, RUN], F32, name=f"wy{h}") for h in range(HALVES)]
+        top_t = [keep.tile([P, PACK, BLOCKS, RUN], F32, name=f"top_t{h}") for h in range(HALVES)]
+
+        def score(c, half):
+            y = y_psum.tile([P, D, P], F32, name="y")
+            for d in range(D):
+                for o in range(PASSES):
+                    nc.tensor.matmul_mx(
+                        y[:, d, :],
+                        lhsT=x_picked[o, half][:, d, :].bitcast(FP8X4),
+                        lhsT_scale=s_dealt[4 * o :, half, d, :],
+                        rhs=h_codes[c][:, o, :].bitcast(FP8X4),
+                        rhs_scale=h_scales[c][:, o, :],
+                        start=(o == 0),
+                        stop=(o == PASSES - 1),
+                    )
+            y_dealt = y[:].rearrange("p d (m t) -> p d t m", t=PACK)
+            squashed = ring.tile([P, D, PACK, RUN], F32, name="squashed")
+            nc.scalar.activation(squashed[:], y_dealt, ACT.Tanh)
+            nc.vector.tensor_reduce(
+                top_t[half][:, :, c, :], y[:].rearrange("p d (m t) -> p t m d", t=PACK), AXIS.X, ALU.max
+            )
+            nc.scalar.activation(ww[half][:, :, :, c, :], squashed[:], ACT.Exp, scale=1.5)
+            nc.vector.tensor_tensor(wy[half][:, :, :, c, :], y_dealt, ww[half][:, :, :, c, :], ALU.mult)
+
+        den = {}
+        num = {}
+
+        def sum_weights(half, slots):
+            bank = sum_psum.tile([P, PACK, P], F32, name="sums")
+            den[half, slots] = bank[:, : len(slots), :]
+            if 2 * len(slots) <= PACK:
+                num[half, slots] = bank[:, len(slots) : 2 * len(slots), :]
+            for n, t in enumerate(slots):
+                for d in range(D):
+                    nc.tensor.matmul(
+                        den[half, slots][:, n, :],
+                        lhsT=ww[half][:, d, t].rearrange("p c m -> p (c m)"),
+                        rhs=ident[:],
+                        is_transpose=True,
+                        start=(d == 0),
+                        stop=(d == D - 1),
+                    )
+
+        def sum_weighted(half, slots):
+            if (half, slots) not in num:
+                bank = sum_psum.tile([P, PACK, P], F32, name="sums")
+                num[half, slots] = bank[:]
+            for n, t in enumerate(slots):
+                for d in range(D):
+                    nc.tensor.matmul(
+                        num[half, slots][:, n, :],
+                        lhsT=wy[half][:, d, t].rearrange("p c m -> p (c m)"),
+                        rhs=ident[:],
+                        is_transpose=True,
+                        start=(d == 0),
+                        stop=(d == D - 1),
+                    )
+
+        def turn_tops(half):
+            tops = top_psum.tile([P, PACK, P], F32, name="tops")
+            for t in range(PACK):
+                nc.tensor.transpose(tops[:, t, :], top_t[half][:, t].rearrange("p c m -> p (c m)"), ident[:])
+            for t in range(PACK):
+                nc.scalar.activation(
+                    top[t][:, half * P : (half + 1) * P], tops[:, t, :], ACT.Copy, scale=unit_knee[:, t : t + 1]
+                )
+
+        def divide(half, slots, engine):
+            width = len(slots) * P // 4
+            parts = den[half, slots].rearrange("p s v -> p (s v)").rearrange("p (h a w) -> p h a w", h=2, a=2)
+            upper = ring.tile([P, 2, width], F32, name="upper")
+            if engine == "scalar":
+                nc.scalar.copy(upper[:], parts[:, 1])
+            else:
+                nc.vector.tensor_copy(upper[:], parts[:, 1])
+            pair = ring.tile([P, 2, width], F32, name="pair")
+            nc.vector.tensor_tensor(pair[:], parts[:, 0], upper[:], ALU.mult)
+            quad = ring.tile([P, width], F32, name="quad")
+            nc.vector.tensor_tensor(quad[:], pair[:, 0, :], pair[:, 1, :], ALU.mult)
+            inv_quad = ring.tile([P, width], F32, name="inv_quad")
+            nc.vector.reciprocal(inv_quad[:], quad[:])
+            inv_pair = ring.tile([P, 2, width], F32, name="inv_pair")
+            nc.vector.tensor_tensor(
+                inv_pair[:], pair[:, ::-1, :], inv_quad[:].unsqueeze(1).to_broadcast([P, 2, width]), ALU.mult
+            )
+            inv = ring.tile([P, 2, 2, width], F32, name="inv")
+            nc.vector.tensor_tensor(
+                inv[:], parts[:, ::-1], inv_pair[:].unsqueeze(1).to_broadcast([P, 2, 2, width]), ALU.mult
+            )
+            inv_flat = inv[:].rearrange("p h a w -> p (h a w)")
+            for n, t in enumerate(slots):
+                nc.vector.tensor_tensor(
+                    bag[t][:, half * P : (half + 1) * P],
+                    num[half, slots][:, n, :],
+                    inv_flat[:, n * P : (n + 1) * P],
+                    ALU.mult,
+                )
+
+        top_pos = {}
+        grown = keep.tile([P, PACK, U], F32, name="grown")
+        factor = keep.tile([P, PACK, U], F32, name="factor")
+        gap = keep.tile([P, PACK, U], F32, name="gap")
+
+        def fetch_top(t, engine):
+            top_pos[t] = ring.tile([P, U], F32, name="top_pos", bufs=3)
+            if engine == "scalar":
+                nc.scalar.activation(top_pos[t][:], top[t][:].indirect(pos_t[:]), ACT.Copy)
+            else:
+                nc.vector.tensor_copy(top_pos[t][:], top[t][:].indirect(pos_t[:]))
+
+        def margin(t, engine):
+            bag_pos = ring.tile([P, U], F32, name="bag_pos", bufs=4)
+            if engine == "scalar":
+                nc.scalar.activation(bag_pos[:], bag[t][:].indirect(pos_t[:]), ACT.Copy)
+            else:
+                nc.vector.tensor_copy(bag_pos[:], bag[t][:].indirect(pos_t[:]))
+            nc.vector.tensor_tensor(gap[:, t, :], bag[t][:].indirect(neg_t[:]), bag_pos[:], ALU.subtract)
+            nc.scalar.activation(grown[:, t, :], gap[:, t, :], ACT.Exp)
+
+        def weigh(t):
+            nc.vector.scalar_tensor_tensor(factor[:, t, :], gap[:, t, :], KNEE, top_pos[t][:], ALU.max, ALU.mult)
+
+        nc.vector.tensor_copy(s_picked[:], s_table[:].indirect(offs_t[:]))
+        nc.vector.tensor_copy(
+            s_dealt[:].rearrange("p h d v -> p h v d"), s_picked[:].rearrange("p (h v d) -> p h v d", h=HALVES, d=D)
+        )
+        for o in range(PASSES):
+            for half in range(HALVES):
+                pick_words(o, half)
+        every = tuple(range(PACK))
+        for c, half in ((0, 0), (1, 0), (2, 0), (3, 0), (0, 1), (1, 1), (2, 1), (3, 1)):
+            if c not in h_codes:
+                quantize_h(c, (("scalar", "scalar"), ("scalar", "scalar"), ("scalar", "vector"), ("scalar", "vector"))[c])
+            score(c, half)
+        sum_weights(0, every)
+        turn_tops(0)
+        sum_weighted(0, every)
+        divide(0, every, "scalar")
+        interleave("scalar", w_grouped[:], w_raw[:])
+        nc.vector.quantize_mx(
+            w_codes[:].bitcast(FP8X4), w_scales[:], w_grouped[:].rearrange("p m j -> p (m j)")
+        )
+
+        groups = ((0, 1), (2, 3))
+        sum_weights(1, groups[0])
+        sum_weighted(1, groups[0])
+        turn_tops(1)
+        divide(1, groups[0], "vector")
+        for g in groups[1:]:
+            sum_weights(1, g)
+            sum_weighted(1, g)
+            divide(1, g, "vector")
+        for t in range(PACK):
+            margin(t, ("scalar","scalar","scalar","scalar")[t])
+        for t in range(PACK):
+            fetch_top(t, ("scalar","scalar","scalar","scalar")[t])
+            weigh(t)
+
+        loss = keep.tile([P, U, PACK], F32, name="loss")
+        factor_grouped = keep.tile([P, U, PACK], F32, name="factor_grouped")
+        hid = keep.tile([P, U, PACK], BF16, name="hid", align_bytes=64)
+        hid_codes = keep.tile([P, U], U32, name="hid_codes", align_bytes=64)
+        hid_scales = keep.tile([P, U], U8, name="hid_scales", align_bytes=64)
+        result = keep.tile([P, U], F32, name="result")
+        capped = keep.tile([P, U, PACK], F32, name="capped")
+        for a, b in PAIR_CHUNKS:
+            nc.vector.tensor_scalar_min(
+                capped[:, a:b, :].rearrange("p (c i) t -> p c t i", i=4),
+                grown[:, :, a:b].rearrange("p t (c i) -> p c t i", i=4),
+                math.exp(KNEE),
+            )
+            interleave("vector", factor_grouped[:, a:b, :], factor[:, :, a:b])
+        for a, b in PAIR_CHUNKS:
+            nc.scalar.activation(loss[:, a:b, :], capped[:, a:b, :], ACT.Ln, bias=1.0)
+            nc.vector.tensor_tensor(hid[:, a:b, :], loss[:, a:b, :], factor_grouped[:, a:b, :], ALU.mult)
+            nc.vector.quantize_mx(
+                hid_codes[:, a:b].bitcast(FP8X4),
+                hid_scales[:, a:b],
+                hid[:, a:b, :].rearrange("p r t -> p (r t)"),
+            )
+            acc = y_psum.tile([P, D, P], F32, name="y")
+            acc_cols = acc[:].rearrange("p d v -> p (d v)")[:, : b - a]
+            nc.tensor.matmul_mx(
+                acc_cols,
+                lhsT=w_codes[:].bitcast(FP8X4),
+                lhsT_scale=w_scales[:],
+                rhs=hid_codes[:, a:b].bitcast(FP8X4),
+                rhs_scale=hid_scales[:, a:b],
+                start=True,
+                stop=True,
+            )
+            nc.scalar.copy(result[:, a:b], acc_cols)
+            nc.sync.dma_start(out[:, a:b], result[:, a:b])

@@ -27,9 +27,9 @@ RUN = P // PACK
 KNEE = 32.0
 BAG_WINDOW = 1024
 TOP_WINDOW = 544
-H_LOADS = ((0, 1), (1, 2), (2, 4))
-UNITS = ((0, 0), (0, 1), (1, 0), (2, 0), (3, 0), (1, 1), (2, 1), (3, 1))
-PAIR_CHUNKS = ((0, 256), (256, 512))
+H_LOADS = ((0, 2), (2, 4))
+UNITS = ((0, 0), (1, 0), (2, 0), (3, 0), (0, 1), (1, 1), (2, 1), (3, 1))
+PAIR_CHUNKS = ((0, 128), (128, 384), (384, 512))
 
 
 def tile_picked_ymilrk_top_p_kernel(
@@ -39,9 +39,8 @@ def tile_picked_ymilrk_top_p_kernel(
     with ExitStack() as ctx:
         keep = ctx.enter_context(tc.tile_pool(name="keep", bufs=1))
         ring = ctx.enter_context(tc.tile_pool(name="ring", bufs=2))
-        y_psum = ctx.enter_context(tc.psum_pool(name="y_psum", bufs=3))
-        sum_psum = ctx.enter_context(tc.psum_pool(name="sum_psum", bufs=4))
-        top_psum = ctx.enter_context(tc.psum_pool(name="top_psum", bufs=1))
+        y_psum = ctx.enter_context(tc.psum_pool(name="y_psum", bufs=4))
+        sum_psum = ctx.enter_context(tc.psum_pool(name="sum_psum", bufs=1))
 
         offs_t = keep.tile([P, S // 16], U16, name="offs_t")
         pos_t = keep.tile([P, U // 16], U16, name="pos_t")
@@ -60,6 +59,13 @@ def tile_picked_ymilrk_top_p_kernel(
                 x_table[o][:, a:b].bitcast(I32), x_words[o, :, a:b].rearrange("p n t -> p (n t)").bitcast(I32)
             )
 
+        def load_scales(o):
+            for q in range(4):
+                nc.sync.dma_start(
+                    s_table[32 * q + 4 * o : 32 * q + 4 * o + 4, :].bitcast(I32),
+                    x_scales[o, 4 * q : 4 * q + 4, :].bitcast(I32),
+                )
+
         def load_h(first, last):
             for o in range(PASSES):
                 rows = hT[o * P * PACK : (o + 1) * P * PACK, first * P : last * P]
@@ -67,13 +73,10 @@ def tile_picked_ymilrk_top_p_kernel(
 
         nc.vector.memset(s_table[:].bitcast(I32), 0)
         load_words(0, 0, T // 2)
-        for q in range(4):
-            nc.sync.dma_start(
-                s_table[32 * q : 32 * q + 4 * PASSES, :].bitcast(I32),
-                x_scales[:, 4 * q : 4 * q + 4, :].bitcast(I32),
-            )
-        nc.sync.dma_start(offs_t[:], offs)
+        load_scales(0)
         load_words(0, T // 2, T)
+        nc.sync.dma_start(offs_t[:], offs)
+        load_scales(1)
         load_words(1, 0, T)
         for first, last in H_LOADS:
             load_h(first, last)
@@ -98,6 +101,8 @@ def tile_picked_ymilrk_top_p_kernel(
             dst = grouped.rearrange("p (c i) j -> p c j i", i=4)
             if engine == "scalar":
                 nc.scalar.copy(dst, src)
+            elif engine == "gpsimd":
+                nc.gpsimd.tensor_scalar(dst, src, 1.0, 0.0, ALU.mult, ALU.add)
             else:
                 nc.vector.tensor_copy(dst, src)
 
@@ -160,77 +165,59 @@ def tile_picked_ymilrk_top_p_kernel(
             nc.scalar.activation(ww[half][:, :, :, c, :], squashed[:], ACT.Exp, scale=1.5)
             nc.vector.tensor_tensor(wy[half][:, :, :, c, :], y_dealt, ww[half][:, :, :, c, :], ALU.mult)
 
-        den = {}
-        num = {}
+        den = [sum_psum.tile([P, 2, HALVES, P], F32, name=f"den{g}") for g in range(2)]
+        num = [sum_psum.tile([P, 2, HALVES, P], F32, name=f"num{g}") for g in range(2)]
 
-        def sum_weights(half, slots):
-            bank = sum_psum.tile([P, PACK, P], F32, name="sums")
-            den[half, slots] = bank[:, : len(slots), :]
-            if 2 * len(slots) <= PACK:
-                num[half, slots] = bank[:, len(slots) : 2 * len(slots), :]
-            for n, t in enumerate(slots):
+        def turn_and_add(bank, src, half, g):
+            for n in range(2):
                 for d in range(D):
                     nc.tensor.matmul(
-                        den[half, slots][:, n, :],
-                        lhsT=ww[half][:, d, t].rearrange("p c m -> p (c m)"),
+                        bank[:, n, half, :],
+                        lhsT=src[:, d, 2 * g + n].rearrange("p c m -> p (c m)"),
                         rhs=ident[:],
                         is_transpose=True,
                         start=(d == 0),
                         stop=(d == D - 1),
                     )
 
-        def sum_weighted(half, slots):
-            if (half, slots) not in num:
-                bank = sum_psum.tile([P, PACK, P], F32, name="sums")
-                num[half, slots] = bank[:]
-            for n, t in enumerate(slots):
-                for d in range(D):
-                    nc.tensor.matmul(
-                        num[half, slots][:, n, :],
-                        lhsT=wy[half][:, d, t].rearrange("p c m -> p (c m)"),
-                        rhs=ident[:],
-                        is_transpose=True,
-                        start=(d == 0),
-                        stop=(d == D - 1),
+        def turn_tops(g):
+            tops = y_psum.tile([P, D, P], F32, name="y")
+            for n in range(2):
+                for half in range(HALVES):
+                    nc.tensor.transpose(
+                        tops[:, 2 * n + half, :], top_t[half][:, 2 * g + n].rearrange("p c m -> p (c m)"), ident[:]
                     )
-
-        def turn_tops(half):
-            tops = top_psum.tile([P, PACK, P], F32, name="tops")
-            for t in range(PACK):
-                nc.tensor.transpose(tops[:, t, :], top_t[half][:, t].rearrange("p c m -> p (c m)"), ident[:])
-            for t in range(PACK):
+            for n in range(2):
+                t = 2 * g + n
                 nc.scalar.activation(
-                    top[t][:, half * P : (half + 1) * P], tops[:, t, :], ACT.Copy, scale=unit_knee[:, t : t + 1]
+                    top[t][:, :V],
+                    tops[:, 2 * n : 2 * n + 2, :].rearrange("p h v -> p (h v)"),
+                    ACT.Copy,
+                    scale=unit_knee[:, t : t + 1],
                 )
 
-        def divide(half, slots, engine):
-            width = len(slots) * P // 4
-            parts = den[half, slots].rearrange("p s v -> p (s v)").rearrange("p (h a w) -> p h a w", h=2, a=2)
-            upper = ring.tile([P, 2, width], F32, name="upper")
-            if engine == "scalar":
-                nc.scalar.copy(upper[:], parts[:, 1])
-            else:
-                nc.vector.tensor_copy(upper[:], parts[:, 1])
-            pair = ring.tile([P, 2, width], F32, name="pair")
-            nc.vector.tensor_tensor(pair[:], parts[:, 0], upper[:], ALU.mult)
-            quad = ring.tile([P, width], F32, name="quad")
+        def divide(g):
+            second = ring.tile([P, HALVES, P], F32, name="second")
+            nc.vector.tensor_copy(second[:], den[g][:, 1])
+            pair = ring.tile([P, HALVES, P], F32, name="pair")
+            nc.vector.tensor_tensor(pair[:], den[g][:, 0], second[:], ALU.mult)
+            quad = ring.tile([P, P], F32, name="quad")
             nc.vector.tensor_tensor(quad[:], pair[:, 0, :], pair[:, 1, :], ALU.mult)
-            inv_quad = ring.tile([P, width], F32, name="inv_quad")
+            inv_quad = ring.tile([P, P], F32, name="inv_quad")
             nc.vector.reciprocal(inv_quad[:], quad[:])
-            inv_pair = ring.tile([P, 2, width], F32, name="inv_pair")
+            inv_pair = ring.tile([P, HALVES, P], F32, name="inv_pair")
             nc.vector.tensor_tensor(
-                inv_pair[:], pair[:, ::-1, :], inv_quad[:].unsqueeze(1).to_broadcast([P, 2, width]), ALU.mult
+                inv_pair[:], pair[:, ::-1, :], inv_quad[:].unsqueeze(1).to_broadcast([P, HALVES, P]), ALU.mult
             )
-            inv = ring.tile([P, 2, 2, width], F32, name="inv")
+            inv = ring.tile([P, 2, HALVES, P], F32, name="inv")
             nc.vector.tensor_tensor(
-                inv[:], parts[:, ::-1], inv_pair[:].unsqueeze(1).to_broadcast([P, 2, 2, width]), ALU.mult
+                inv[:], den[g][:, ::-1], inv_pair[:].unsqueeze(1).to_broadcast([P, 2, HALVES, P]), ALU.mult
             )
-            inv_flat = inv[:].rearrange("p h a w -> p (h a w)")
-            for n, t in enumerate(slots):
+            for n in range(2):
                 nc.vector.tensor_tensor(
-                    bag[t][:, half * P : (half + 1) * P],
-                    num[half, slots][:, n, :],
-                    inv_flat[:, n * P : (n + 1) * P],
+                    bag[2 * g + n][:, :V],
+                    num[g][:, n].rearrange("p h v -> p (h v)"),
+                    inv[:, n].rearrange("p h v -> p (h v)"),
                     ALU.mult,
                 )
 
@@ -240,7 +227,7 @@ def tile_picked_ymilrk_top_p_kernel(
         gap = keep.tile([P, PACK, U], F32, name="gap")
 
         def fetch_top(t, engine):
-            top_pos[t] = ring.tile([P, U], F32, name="top_pos", bufs=3)
+            top_pos[t] = ring.tile([P, U], F32, name="top_pos", bufs=4)
             if engine == "scalar":
                 nc.scalar.activation(top_pos[t][:], top[t][:].indirect(pos_t[:]), ACT.Copy)
             else:
@@ -265,52 +252,47 @@ def tile_picked_ymilrk_top_p_kernel(
         for o in range(PASSES):
             for half in range(HALVES):
                 pick_words(o, half)
-        every = tuple(range(PACK))
-        for c, half in ((0, 0), (1, 0), (2, 0), (3, 0), (0, 1), (1, 1), (2, 1), (3, 1)):
+        for c, half in UNITS:
             if c not in h_codes:
                 quantize_h(c, (("scalar", "scalar"), ("scalar", "scalar"), ("scalar", "vector"), ("scalar", "vector"))[c])
             score(c, half)
-        sum_weights(0, every)
-        turn_tops(0)
-        sum_weighted(0, every)
-        divide(0, every, "scalar")
-        interleave("scalar", w_grouped[:], w_raw[:])
+        interleave("gpsimd", w_grouped[:], w_raw[:])
         nc.vector.quantize_mx(
             w_codes[:].bitcast(FP8X4), w_scales[:], w_grouped[:].rearrange("p m j -> p (m j)")
         )
-
-        groups = ((0, 1), (2, 3))
-        sum_weights(1, groups[0])
-        sum_weighted(1, groups[0])
-        turn_tops(1)
-        divide(1, groups[0], "vector")
-        for g in groups[1:]:
-            sum_weights(1, g)
-            sum_weighted(1, g)
-            divide(1, g, "vector")
+        for half in range(HALVES):
+            for g in range(2):
+                turn_and_add(den[g], ww[half], half, g)
+        for g in range(2):
+            turn_tops(g)
+            for half in range(HALVES):
+                turn_and_add(num[g], wy[half], half, g)
+        for g in range(2):
+            divide(g)
         for t in range(PACK):
             margin(t, ("scalar","scalar","scalar","scalar")[t])
         for t in range(PACK):
             fetch_top(t, ("scalar","scalar","scalar","scalar")[t])
-            weigh(t)
 
-        loss = keep.tile([P, U, PACK], F32, name="loss")
-        factor_grouped = keep.tile([P, U, PACK], F32, name="factor_grouped")
+
+        loss = keep.tile([P, PACK, U], F32, name="loss")
+        capped = keep.tile([P, PACK, U], F32, name="capped")
         hid = keep.tile([P, U, PACK], BF16, name="hid", align_bytes=64)
         hid_codes = keep.tile([P, U], U32, name="hid_codes", align_bytes=64)
         hid_scales = keep.tile([P, U], U8, name="hid_scales", align_bytes=64)
         result = keep.tile([P, U], F32, name="result")
-        capped = keep.tile([P, U, PACK], F32, name="capped")
+        for a, b in ((0, 2), (2, 4)):
+            nc.vector.tensor_scalar_min(capped[:, a:b, :], grown[:, a:b, :], math.exp(KNEE))
+        for t in range(PACK):
+            weigh(t)
         for a, b in PAIR_CHUNKS:
-            nc.vector.tensor_scalar_min(
-                capped[:, a:b, :].rearrange("p (c i) t -> p c t i", i=4),
-                grown[:, :, a:b].rearrange("p t (c i) -> p c t i", i=4),
-                math.exp(KNEE),
+            nc.scalar.activation(loss[:, :, a:b], capped[:, :, a:b], ACT.Ln, bias=1.0)
+            nc.vector.tensor_tensor(
+                hid[:, a:b, :].rearrange("p (c i) t -> p c t i", i=4),
+                loss[:, :, a:b].rearrange("p t (c i) -> p c t i", i=4),
+                factor[:, :, a:b].rearrange("p t (c i) -> p c t i", i=4),
+                ALU.mult,
             )
-            interleave("vector", factor_grouped[:, a:b, :], factor[:, :, a:b])
-        for a, b in PAIR_CHUNKS:
-            nc.scalar.activation(loss[:, a:b, :], capped[:, a:b, :], ACT.Ln, bias=1.0)
-            nc.vector.tensor_tensor(hid[:, a:b, :], loss[:, a:b, :], factor_grouped[:, a:b, :], ALU.mult)
             nc.vector.quantize_mx(
                 hid_codes[:, a:b].bitcast(FP8X4),
                 hid_scales[:, a:b],

@@ -29,7 +29,7 @@ BAG_WINDOW = 1024
 TOP_WINDOW = 544
 H_LOADS = ((0, 2), (2, 4))
 UNITS = ((0, 0), (1, 0), (2, 0), (3, 0), (0, 1), (1, 1), (2, 1), (3, 1))
-PAIR_CHUNKS = ((0, 128), (128, 384), (384, 512))
+PAIR_CHUNKS = ((0, 128), (128, 256), (256, 384), (384, 512))
 
 
 def tile_picked_ymilrk_top_p_kernel(
@@ -93,12 +93,9 @@ def tile_picked_ymilrk_top_p_kernel(
             nc.vector.memset(bag[t][:, V:], 0.0)
             nc.vector.memset(top[t][:, V:], 0.0)
 
-        unit_knee = keep.tile([P, PACK], F32, name="unit_knee")
-        nc.scalar.mul(unit_knee[:], unit_raw[:], 1.0 / KNEE)
-
         def interleave(engine, grouped, raw):
-            src = raw.rearrange("p j (c i) -> p c j i", i=4)
-            dst = grouped.rearrange("p (c i) j -> p c j i", i=4)
+            src = raw.rearrange("p j (c i) -> p c j i", i=2)
+            dst = grouped.rearrange("p (c i) j -> p c j i", i=2)
             if engine == "scalar":
                 nc.scalar.copy(dst, src)
             elif engine == "gpsimd":
@@ -193,7 +190,7 @@ def tile_picked_ymilrk_top_p_kernel(
                     top[t][:, :V],
                     tops[:, 2 * n : 2 * n + 2, :].rearrange("p h v -> p (h v)"),
                     ACT.Copy,
-                    scale=unit_knee[:, t : t + 1],
+                    scale=unit_raw[:, t : t + 1],
                 )
 
         def divide(g):
@@ -202,7 +199,7 @@ def tile_picked_ymilrk_top_p_kernel(
             pair = ring.tile([P, HALVES, P], F32, name="pair")
             nc.vector.tensor_tensor(pair[:], den[g][:, 0], second[:], ALU.mult)
             quad = ring.tile([P, P], F32, name="quad")
-            nc.vector.tensor_tensor(quad[:], pair[:, 0, :], pair[:, 1, :], ALU.mult)
+            nc.vector.scalar_tensor_tensor(quad[:], pair[:, 0, :], KNEE, pair[:, 1, :], ALU.mult, ALU.mult)
             inv_quad = ring.tile([P, P], F32, name="inv_quad")
             nc.vector.reciprocal(inv_quad[:], quad[:])
             inv_pair = ring.tile([P, HALVES, P], F32, name="inv_pair")
@@ -240,10 +237,10 @@ def tile_picked_ymilrk_top_p_kernel(
             else:
                 nc.vector.tensor_copy(bag_pos[:], bag[t][:].indirect(pos_t[:]))
             nc.vector.tensor_tensor(gap[:, t, :], bag[t][:].indirect(neg_t[:]), bag_pos[:], ALU.subtract)
-            nc.scalar.activation(grown[:, t, :], gap[:, t, :], ACT.Exp)
+            nc.scalar.activation(grown[:, t, :], gap[:, t, :], ACT.Exp, scale=KNEE)
 
         def weigh(t):
-            nc.vector.scalar_tensor_tensor(factor[:, t, :], gap[:, t, :], KNEE, top_pos[t][:], ALU.max, ALU.mult)
+            nc.vector.scalar_tensor_tensor(factor[:, t, :], gap[:, t, :], 1.0, top_pos[t][:], ALU.max, ALU.mult)
 
         nc.vector.tensor_copy(s_picked[:], s_table[:].indirect(offs_t[:]))
         nc.vector.tensor_copy(
@@ -254,9 +251,9 @@ def tile_picked_ymilrk_top_p_kernel(
                 pick_words(o, half)
         for c, half in UNITS:
             if c not in h_codes:
-                quantize_h(c, (("scalar", "scalar"), ("scalar", "scalar"), ("scalar", "vector"), ("scalar", "vector"))[c])
+                quantize_h(c, (("scalar", "scalar"), ("scalar", "scalar"), ("scalar", "scalar"), ("scalar", "vector"))[c])
             score(c, half)
-        interleave("gpsimd", w_grouped[:], w_raw[:])
+        interleave("scalar", w_grouped[:], w_raw[:])
         nc.vector.quantize_mx(
             w_codes[:].bitcast(FP8X4), w_scales[:], w_grouped[:].rearrange("p m j -> p (m j)")
         )
@@ -288,9 +285,9 @@ def tile_picked_ymilrk_top_p_kernel(
         for a, b in PAIR_CHUNKS:
             nc.scalar.activation(loss[:, :, a:b], capped[:, :, a:b], ACT.Ln, bias=1.0)
             nc.vector.tensor_tensor(
-                hid[:, a:b, :].rearrange("p (c i) t -> p c t i", i=4),
-                loss[:, :, a:b].rearrange("p t (c i) -> p c t i", i=4),
-                factor[:, :, a:b].rearrange("p t (c i) -> p c t i", i=4),
+                hid[:, a:b, :].rearrange("p (c i) t -> p c t i", i=2),
+                loss[:, :, a:b].rearrange("p t (c i) -> p c t i", i=2),
+                factor[:, :, a:b].rearrange("p t (c i) -> p c t i", i=2),
                 ALU.mult,
             )
             nc.vector.quantize_mx(

@@ -244,7 +244,7 @@ def tile_picked_ymilrk_top_p_kernel(
 
         nc.vector.tensor_copy(s_picked[:], s_table[:].indirect(offs_t[:]))
         nc.vector.tensor_copy(
-            s_dealt[:].rearrange("p h d v -> p h v d"), s_picked[:].rearrange("p (h v d) -> p h v d", h=HALVES, d=D)
+            s_dealt[:], s_picked[:].rearrange("p (h v d) -> p h d v", h=HALVES, d=D)
         )
         for o in range(PASSES):
             for half in range(HALVES):

@@ -21,15 +21,20 @@ AXIS = mybir.AxisListType
 P = 128
 PACK = 4
 PASSES = K // (P * PACK)
+QUADRANTS = 4
+SCALE_ROWS = 4
+LIST_ROWS = 16
 HALVES = V // P
 BLOCKS = H // P
 RUN = P // PACK
+GROUPS = 2
+LOAD_BLOCKS = 2
 KNEE = 32.0
 BAG_WINDOW = 1024
-TOP_WINDOW = 544
-H_LOADS = ((0, 2), (2, 4))
-UNITS = ((0, 0), (1, 0), (2, 0), (3, 0), (0, 1), (1, 1), (2, 1), (3, 1))
-PAIR_CHUNKS = ((0, 128), (128, 256), (256, 384), (384, 512))
+TOP_WINDOW = 704
+PAIR_CHUNK = 128
+Y_BANKS = 4
+TOP_ON_VECTOR = (U, U, U // 2, U // 2)
 
 
 def tile_picked_ymilrk_top_p_kernel(
@@ -39,48 +44,46 @@ def tile_picked_ymilrk_top_p_kernel(
     with ExitStack() as ctx:
         keep = ctx.enter_context(tc.tile_pool(name="keep", bufs=1))
         ring = ctx.enter_context(tc.tile_pool(name="ring", bufs=2))
-        y_psum = ctx.enter_context(tc.psum_pool(name="y_psum", bufs=4))
+        y_psum = ctx.enter_context(tc.psum_pool(name="y_psum", bufs=Y_BANKS))
         sum_psum = ctx.enter_context(tc.psum_pool(name="sum_psum", bufs=1))
 
-        offs_t = keep.tile([P, S // 16], U16, name="offs_t")
-        pos_t = keep.tile([P, U // 16], U16, name="pos_t")
-        neg_t = keep.tile([P, U // 16], U16, name="neg_t")
-        x_table = [keep.tile([P, T], U32, name=f"x_table{o}") for o in range(PASSES)]
-        s_table = keep.tile([P, T], U8, name="s_table")
+        offs_t = keep.tile([P, S // LIST_ROWS], U16, name="offs_t")
+        pos_t = keep.tile([P, U // LIST_ROWS], U16, name="pos_t")
+        neg_t = keep.tile([P, U // LIST_ROWS], U16, name="neg_t")
+        word_table = [keep.tile([P, T], U32, name=f"word_table{o}") for o in range(PASSES)]
+        scale_table = keep.tile([P, T], U8, name="scale_table")
         h_raw = {}
-        for first, last in H_LOADS:
+        for first in range(0, BLOCKS, LOAD_BLOCKS):
             for o in range(PASSES):
-                h_raw[first, o] = keep.tile([P, PACK, (last - first) * P], F32, name=f"h_raw{first}_{o}")
-        unit_raw = keep.tile([P, PACK], F32, name="unit_raw")
+                h_raw[first, o] = keep.tile([P, PACK, LOAD_BLOCKS * P], F32, name=f"h_raw{first}_{o}")
+        unit_t = keep.tile([P, PACK], F32, name="unit_t")
         w_raw = keep.tile([P, PACK, N], F32, name="w_raw")
 
         def load_words(o, a, b):
             nc.sync.dma_start(
-                x_table[o][:, a:b].bitcast(I32), x_words[o, :, a:b].rearrange("p n t -> p (n t)").bitcast(I32)
+                word_table[o][:, a:b].bitcast(I32), x_words[o, :, a:b].rearrange("p n t -> p (n t)").bitcast(I32)
             )
 
         def load_scales(o):
-            for q in range(4):
+            for q in range(QUADRANTS):
+                row = 32 * q + SCALE_ROWS * o
                 nc.sync.dma_start(
-                    s_table[32 * q + 4 * o : 32 * q + 4 * o + 4, :].bitcast(I32),
-                    x_scales[o, 4 * q : 4 * q + 4, :].bitcast(I32),
+                    scale_table[row : row + SCALE_ROWS, :].bitcast(I32),
+                    x_scales[o, SCALE_ROWS * q : SCALE_ROWS * (q + 1), :].bitcast(I32),
                 )
 
-        def load_h(first, last):
-            for o in range(PASSES):
-                rows = hT[o * P * PACK : (o + 1) * P * PACK, first * P : last * P]
-                nc.sync.dma_start(h_raw[first, o][:], rows.rearrange("(p j) n -> p j n", j=PACK))
-
-        nc.vector.memset(s_table[:].bitcast(I32), 0)
+        nc.vector.memset(scale_table[:].bitcast(I32), 0)
         load_words(0, 0, T // 2)
         load_scales(0)
         load_words(0, T // 2, T)
         nc.sync.dma_start(offs_t[:], offs)
         load_scales(1)
         load_words(1, 0, T)
-        for first, last in H_LOADS:
-            load_h(first, last)
-        nc.sync.dma_start(unit_raw[:], unit.rearrange("(p t) one -> p (t one)", t=PACK))
+        for first in range(0, BLOCKS, LOAD_BLOCKS):
+            for o in range(PASSES):
+                rows = hT[o * P * PACK : (o + 1) * P * PACK, first * P : (first + LOAD_BLOCKS) * P]
+                nc.sync.dma_start(h_raw[first, o][:], rows.rearrange("(p j) n -> p j n", j=PACK))
+        nc.sync.dma_start(unit_t[:], unit.rearrange("(p t) one -> p (t one)", t=PACK))
         nc.sync.dma_start(pos_t[:], pos)
         nc.sync.dma_start(neg_t[:], neg)
         nc.sync.dma_start(w_raw[:], w1.rearrange("(p j) m -> p j m", j=PACK))
@@ -93,84 +96,89 @@ def tile_picked_ymilrk_top_p_kernel(
             nc.vector.memset(bag[t][:, V:], 0.0)
             nc.vector.memset(top[t][:, V:], 0.0)
 
-        def interleave(engine, grouped, raw):
-            src = raw.rearrange("p j (c i) -> p c j i", i=2)
-            dst = grouped.rearrange("p (c i) j -> p c j i", i=2)
-            if engine == "scalar":
-                nc.scalar.copy(dst, src)
-            elif engine == "gpsimd":
-                nc.gpsimd.tensor_scalar(dst, src, 1.0, 0.0, ALU.mult, ALU.add)
-            else:
-                nc.vector.tensor_copy(dst, src)
+        def from_rows(rows):
+            return rows.rearrange("p j (c i) -> p c j i", i=2)
 
-        w_grouped = keep.tile([P, N, PACK], BF16, name="w_grouped", align_bytes=64)
-        w_codes = keep.tile([P, N], U32, name="w_codes", align_bytes=64)
-        w_scales = keep.tile([P, N], U8, name="w_scales", align_bytes=64)
+        def to_words(grouped):
+            return grouped.rearrange("p (c i) j -> p c j i", i=2)
 
-        s_picked = keep.tile([P, S], U8, name="s_picked")
-        s_dealt = keep.tile([P, HALVES, D, P], U8, name="s_dealt", align_bytes=64)
-        x_picked = {}
-
-        def pick_words(o, half):
-            x_picked[o, half] = keep.tile([P, D, P], U32, name=f"x_picked{o}_{half}", align_bytes=64)
-            cols = S // 16 // HALVES
-            nc.vector.tensor_copy(
-                x_picked[o, half][:].rearrange("p d v -> p v d"),
-                x_table[o][:].indirect(offs_t[:, half * cols : (half + 1) * cols]),
-            )
+        scales_picked = keep.tile([P, S], U8, name="scales_picked")
+        scales_dealt = keep.tile([P, HALVES, D, P], U8, name="scales_dealt", align_bytes=64)
+        nc.vector.tensor_copy(scales_picked[:], scale_table[:].indirect(offs_t[:]))
+        nc.vector.tensor_copy(scales_dealt[:], scales_picked[:].rearrange("p (h v d) -> p h d v", h=HALVES, d=D))
+        words_dealt = {}
+        list_cols = S // LIST_ROWS // HALVES
+        for o in range(PASSES):
+            for half in range(HALVES):
+                words_dealt[o, half] = keep.tile([P, D, P], U32, name=f"words_dealt{o}_{half}", align_bytes=64)
+                nc.vector.tensor_copy(
+                    words_dealt[o, half][:].rearrange("p d v -> p v d"),
+                    word_table[o][:].indirect(offs_t[:, half * list_cols : (half + 1) * list_cols]),
+                )
 
         h_codes = {}
         h_scales = {}
 
-        def quantize_h(c, engines):
-            first = max(f for f, last in H_LOADS if f <= c)
+        def quantize_h(c):
+            first = c - c % LOAD_BLOCKS
             cols = slice((c - first) * P, (c - first + 1) * P)
             grouped = keep.tile([P, PASSES, P, PACK], BF16, name=f"h_grouped{c}", align_bytes=64)
             h_codes[c] = keep.tile([P, PASSES, P], U32, name=f"h_codes{c}", align_bytes=64)
             h_scales[c] = keep.tile([P, PASSES, P], U8, name=f"h_scales{c}", align_bytes=64)
             for o in range(PASSES):
-                interleave(engines[o], grouped[:, o], h_raw[first, o][:, :, cols])
+                last_load = first + LOAD_BLOCKS == BLOCKS and o == PASSES - 1
+                cast = nc.vector.tensor_copy if last_load else nc.scalar.copy
+                cast(to_words(grouped[:, o]), from_rows(h_raw[first, o][:, :, cols]))
             nc.vector.quantize_mx(
                 h_codes[c][:].rearrange("p o n -> p (o n)").bitcast(FP8X4),
                 h_scales[c][:].rearrange("p o n -> p (o n)"),
                 grouped[:].rearrange("p o n j -> p (o n j)"),
             )
 
-        ww = [keep.tile([P, D, PACK, BLOCKS, RUN], F32, name=f"ww{h}") for h in range(HALVES)]
-        wy = [keep.tile([P, D, PACK, BLOCKS, RUN], F32, name=f"wy{h}") for h in range(HALVES)]
-        top_t = [keep.tile([P, PACK, BLOCKS, RUN], F32, name=f"top_t{h}") for h in range(HALVES)]
+        ww = [
+            keep.tile([P, D, PACK, BLOCKS, RUN], F32, name=f"ww{half}", tag=f"ww{half}", align_bytes=64)
+            for half in range(HALVES)
+        ]
+        wy = [keep.tile([P, D, PACK, BLOCKS, RUN], F32, name=f"wy{half}") for half in range(HALVES)]
+        top_turned = [keep.tile([P, PACK, BLOCKS, RUN], F32, name=f"top_turned{half}") for half in range(HALVES)]
 
         def score(c, half):
-            y = y_psum.tile([P, D, P], F32, name="y")
+            y = y_psum.tile([P, D, P], F32, name="bank")
             for d in range(D):
                 for o in range(PASSES):
                     nc.tensor.matmul_mx(
                         y[:, d, :],
-                        lhsT=x_picked[o, half][:, d, :].bitcast(FP8X4),
-                        lhsT_scale=s_dealt[4 * o :, half, d, :],
+                        lhsT=words_dealt[o, half][:, d, :].bitcast(FP8X4),
+                        lhsT_scale=scales_dealt[SCALE_ROWS * o :, half, d, :],
                         rhs=h_codes[c][:, o, :].bitcast(FP8X4),
                         rhs_scale=h_scales[c][:, o, :],
                         start=(o == 0),
                         stop=(o == PASSES - 1),
                     )
-            y_dealt = y[:].rearrange("p d (m t) -> p d t m", t=PACK)
+            y_by_slot = y[:].rearrange("p d (m t) -> p d t m", t=PACK)
             squashed = ring.tile([P, D, PACK, RUN], F32, name="squashed")
-            nc.scalar.activation(squashed[:], y_dealt, ACT.Tanh)
+            nc.scalar.activation(squashed[:], y_by_slot, ACT.Tanh)
             nc.vector.tensor_reduce(
-                top_t[half][:, :, c, :], y[:].rearrange("p d (m t) -> p t m d", t=PACK), AXIS.X, ALU.max
+                top_turned[half][:, :, c, :], y[:].rearrange("p d (m t) -> p t m d", t=PACK), AXIS.X, ALU.max
             )
             nc.scalar.activation(ww[half][:, :, :, c, :], squashed[:], ACT.Exp, scale=1.5)
-            nc.vector.tensor_tensor(wy[half][:, :, :, c, :], y_dealt, ww[half][:, :, :, c, :], ALU.mult)
+            nc.vector.tensor_tensor(wy[half][:, :, :, c, :], y_by_slot, ww[half][:, :, :, c, :], ALU.mult)
 
-        den = [sum_psum.tile([P, 2, HALVES, P], F32, name=f"den{g}") for g in range(2)]
-        num = [sum_psum.tile([P, 2, HALVES, P], F32, name=f"num{g}") for g in range(2)]
+        for half in range(HALVES):
+            for c in range(BLOCKS):
+                if half == 0:
+                    quantize_h(c)
+                score(c, half)
 
-        def turn_and_add(bank, src, half, g):
+        den = [sum_psum.tile([P, 2, HALVES, P], F32, name=f"den{g}") for g in range(GROUPS)]
+        num = [sum_psum.tile([P, 2, HALVES, P], F32, name=f"num{g}") for g in range(GROUPS)]
+
+        def turn_and_add(bank, members, half, g):
             for n in range(2):
                 for d in range(D):
                     nc.tensor.matmul(
                         bank[:, n, half, :],
-                        lhsT=src[:, d, 2 * g + n].rearrange("p c m -> p (c m)"),
+                        lhsT=members[:, d, 2 * g + n].rearrange("p c m -> p (c m)"),
                         rhs=ident[:],
                         is_transpose=True,
                         start=(d == 0),
@@ -178,133 +186,99 @@ def tile_picked_ymilrk_top_p_kernel(
                     )
 
         def turn_tops(g):
-            tops = y_psum.tile([P, D, P], F32, name="y")
+            bank = y_psum.tile([P, D, P], F32, name="bank")
             for n in range(2):
                 for half in range(HALVES):
                     nc.tensor.transpose(
-                        tops[:, 2 * n + half, :], top_t[half][:, 2 * g + n].rearrange("p c m -> p (c m)"), ident[:]
+                        bank[:, 2 * n + half, :],
+                        top_turned[half][:, 2 * g + n].rearrange("p c m -> p (c m)"),
+                        ident[:],
                     )
             for n in range(2):
                 t = 2 * g + n
-                nc.scalar.activation(
-                    top[t][:, :V],
-                    tops[:, 2 * n : 2 * n + 2, :].rearrange("p h v -> p (h v)"),
-                    ACT.Copy,
-                    scale=unit_raw[:, t : t + 1],
+                nc.vector.tensor_scalar_mul(
+                    top[t][:, :V], bank[:, 2 * n : 2 * n + 2, :].rearrange("p h v -> p (h v)"), unit_t[:, t : t + 1]
                 )
 
-        def divide(g):
-            second = ring.tile([P, HALVES, P], F32, name="second")
-            nc.vector.tensor_copy(second[:], den[g][:, 1])
-            pair = ring.tile([P, HALVES, P], F32, name="pair")
-            nc.vector.tensor_tensor(pair[:], den[g][:, 0], second[:], ALU.mult)
-            quad = ring.tile([P, P], F32, name="quad")
-            nc.vector.scalar_tensor_tensor(quad[:], pair[:, 0, :], KNEE, pair[:, 1, :], ALU.mult, ALU.mult)
-            inv_quad = ring.tile([P, P], F32, name="inv_quad")
-            nc.vector.reciprocal(inv_quad[:], quad[:])
-            inv_pair = ring.tile([P, HALVES, P], F32, name="inv_pair")
-            nc.vector.tensor_tensor(
-                inv_pair[:], pair[:, ::-1, :], inv_quad[:].unsqueeze(1).to_broadcast([P, HALVES, P]), ALU.mult
-            )
-            inv = ring.tile([P, 2, HALVES, P], F32, name="inv")
-            nc.vector.tensor_tensor(
-                inv[:], den[g][:, ::-1], inv_pair[:].unsqueeze(1).to_broadcast([P, 2, HALVES, P]), ALU.mult
-            )
-            for n in range(2):
-                nc.vector.tensor_tensor(
-                    bag[2 * g + n][:, :V],
-                    num[g][:, n].rearrange("p h v -> p (h v)"),
-                    inv[:, n].rearrange("p h v -> p (h v)"),
-                    ALU.mult,
-                )
-
-        top_pos = {}
-        grown = keep.tile([P, PACK, U], F32, name="grown")
-        factor = keep.tile([P, PACK, U], F32, name="factor")
-        gap = keep.tile([P, PACK, U], F32, name="gap")
-
-        def fetch_top(t, engine):
-            top_pos[t] = ring.tile([P, U], F32, name="top_pos", bufs=4)
-            if engine == "scalar":
-                nc.scalar.activation(top_pos[t][:], top[t][:].indirect(pos_t[:]), ACT.Copy)
-            else:
-                nc.vector.tensor_copy(top_pos[t][:], top[t][:].indirect(pos_t[:]))
-
-        def margin(t, engine):
-            bag_pos = ring.tile([P, U], F32, name="bag_pos", bufs=4)
-            if engine == "scalar":
-                nc.scalar.activation(bag_pos[:], bag[t][:].indirect(pos_t[:]), ACT.Copy)
-            else:
-                nc.vector.tensor_copy(bag_pos[:], bag[t][:].indirect(pos_t[:]))
-            nc.vector.tensor_tensor(gap[:, t, :], bag[t][:].indirect(neg_t[:]), bag_pos[:], ALU.subtract)
-            nc.scalar.activation(grown[:, t, :], gap[:, t, :], ACT.Exp, scale=KNEE)
-
-        def weigh(t):
-            nc.vector.scalar_tensor_tensor(factor[:, t, :], gap[:, t, :], 1.0, top_pos[t][:], ALU.max, ALU.mult)
-
-        nc.vector.tensor_copy(s_picked[:], s_table[:].indirect(offs_t[:]))
-        nc.vector.tensor_copy(
-            s_dealt[:], s_picked[:].rearrange("p (h v d) -> p h d v", h=HALVES, d=D)
-        )
-        for o in range(PASSES):
-            for half in range(HALVES):
-                pick_words(o, half)
-        for c, half in UNITS:
-            if c not in h_codes:
-                quantize_h(c, (("scalar", "scalar"), ("scalar", "scalar"), ("scalar", "scalar"), ("scalar", "vector"))[c])
-            score(c, half)
-        interleave("scalar", w_grouped[:], w_raw[:])
-        nc.vector.quantize_mx(
-            w_codes[:].bitcast(FP8X4), w_scales[:], w_grouped[:].rearrange("p m j -> p (m j)")
-        )
         for half in range(HALVES):
-            for g in range(2):
+            for g in range(GROUPS):
                 turn_and_add(den[g], ww[half], half, g)
-        for g in range(2):
+        for g in range(GROUPS):
             turn_tops(g)
             for half in range(HALVES):
                 turn_and_add(num[g], wy[half], half, g)
-        for g in range(2):
-            divide(g)
-        for t in range(PACK):
-            margin(t, ("scalar","scalar","scalar","scalar")[t])
-        for t in range(PACK):
-            fetch_top(t, ("scalar","scalar","scalar","scalar")[t])
 
+        log_den = keep.tile([P, GROUPS, 2 * V], F32, name="log_den", tag="log_den")
+        inv_den = keep.tile([P, GROUPS, 2 * V], F32, name="inv_den")
+        for g in range(GROUPS):
+            nc.scalar.activation(log_den[:, g, :], den[g][:].rearrange("p n h v -> p (n h v)"), ACT.Ln)
+        for n in range(2):
+            cols = slice(n * V, (n + 1) * V)
+            nc.scalar.activation(inv_den[:, :, cols], log_den[:, :, cols], ACT.Exp, scale=-1.0)
+            for g in range(GROUPS):
+                nc.vector.scalar_tensor_tensor(
+                    bag[2 * g + n][:, :V],
+                    num[g][:, n].rearrange("p h v -> p (h v)"),
+                    1.0 / KNEE,
+                    inv_den[:, g, cols],
+                    ALU.mult,
+                    ALU.mult,
+                )
+        slots_as_made = [2 * g + n for n in range(2) for g in range(GROUPS)]
 
-        loss = keep.tile([P, PACK, U], F32, name="loss")
+        bag_pos = keep.tile([P, PACK, U], F32, name="bag_pos")
+        gap = keep.tile([P, PACK, U], F32, name="gap")
+        grown = keep.tile([P, PACK, U], F32, name="grown")
+        for t in slots_as_made:
+            nc.scalar.activation(bag_pos[:, t, :], bag[t][:].indirect(pos_t[:]), ACT.Copy)
+        for t in slots_as_made:
+            nc.vector.tensor_tensor(gap[:, t, :], bag[t][:].indirect(neg_t[:]), bag_pos[:, t, :], ALU.subtract)
+            nc.scalar.activation(grown[:, t, :], gap[:, t, :], ACT.Exp, scale=KNEE)
+
+        top_pos = {}
+        for t in range(PACK):
+            tag = "log_den" if t == PACK - 1 else f"top_pos{t}"
+            top_pos[t] = keep.tile([P, U], F32, name="top_pos", tag=tag)
+            cut = TOP_ON_VECTOR[t]
+            nc.vector.tensor_copy(top_pos[t][:, :cut], top[t][:].indirect(pos_t[:, : cut // LIST_ROWS]))
+            if cut < U:
+                nc.scalar.activation(top_pos[t][:, cut:], top[t][:].indirect(pos_t[:, cut // LIST_ROWS :]), ACT.Copy)
+
+        w_grouped = keep.tile([P, N, PACK], BF16, name="w_grouped", tag="ww0", align_bytes=64)
+        w_codes = keep.tile([P, N], U32, name="w_codes", align_bytes=64)
+        w_scales = keep.tile([P, N], U8, name="w_scales", align_bytes=64)
+        nc.gpsimd.tensor_scalar(to_words(w_grouped[:]), from_rows(w_raw[:]), 1.0, 0.0, ALU.mult, ALU.add)
+        nc.vector.quantize_mx(w_codes[:].bitcast(FP8X4), w_scales[:], w_grouped[:].rearrange("p m j -> p (m j)"))
+
         capped = keep.tile([P, PACK, U], F32, name="capped")
+        factor = keep.tile([P, PACK, U], F32, name="factor")
+        loss = keep.tile([P, PACK, U], F32, name="loss")
         hid = keep.tile([P, U, PACK], BF16, name="hid", align_bytes=64)
         hid_codes = keep.tile([P, U], U32, name="hid_codes", align_bytes=64)
         hid_scales = keep.tile([P, U], U8, name="hid_scales", align_bytes=64)
         result = keep.tile([P, U], F32, name="result")
-        for a, b in ((0, 2), (2, 4)):
-            nc.vector.tensor_scalar_min(capped[:, a:b, :], grown[:, a:b, :], math.exp(KNEE))
+        for slots in (slice(0, PACK - 1), slice(PACK - 1, PACK)):
+            nc.vector.tensor_scalar_min(capped[:, slots, :], grown[:, slots, :], math.exp(KNEE))
         for t in range(PACK):
-            weigh(t)
-        for a, b in PAIR_CHUNKS:
-            nc.scalar.activation(loss[:, :, a:b], capped[:, :, a:b], ACT.Ln, bias=1.0)
+            nc.vector.scalar_tensor_tensor(factor[:, t, :], gap[:, t, :], 1.0, top_pos[t][:], ALU.max, ALU.mult)
+        for a in range(0, U, PAIR_CHUNK):
+            pairs = slice(a, a + PAIR_CHUNK)
+            nc.scalar.activation(loss[:, :, pairs], capped[:, :, pairs], ACT.Ln, bias=1.0)
             nc.vector.tensor_tensor(
-                hid[:, a:b, :].rearrange("p (c i) t -> p c t i", i=2),
-                loss[:, :, a:b].rearrange("p t (c i) -> p c t i", i=2),
-                factor[:, :, a:b].rearrange("p t (c i) -> p c t i", i=2),
-                ALU.mult,
+                to_words(hid[:, pairs, :]), from_rows(loss[:, :, pairs]), from_rows(factor[:, :, pairs]), ALU.mult
             )
             nc.vector.quantize_mx(
-                hid_codes[:, a:b].bitcast(FP8X4),
-                hid_scales[:, a:b],
-                hid[:, a:b, :].rearrange("p r t -> p (r t)"),
+                hid_codes[:, pairs].bitcast(FP8X4), hid_scales[:, pairs], hid[:, pairs, :].rearrange("p r t -> p (r t)")
             )
-            acc = y_psum.tile([P, D, P], F32, name="y")
-            acc_cols = acc[:].rearrange("p d v -> p (d v)")[:, : b - a]
+            bank = y_psum.tile([P, D, P], F32, name="bank")
             nc.tensor.matmul_mx(
-                acc_cols,
+                bank[:, 0, :],
                 lhsT=w_codes[:].bitcast(FP8X4),
                 lhsT_scale=w_scales[:],
-                rhs=hid_codes[:, a:b].bitcast(FP8X4),
-                rhs_scale=hid_scales[:, a:b],
+                rhs=hid_codes[:, pairs].bitcast(FP8X4),
+                rhs_scale=hid_scales[:, pairs],
                 start=True,
                 stop=True,
             )
-            nc.scalar.copy(result[:, a:b], acc_cols)
-            nc.sync.dma_start(out[:, a:b], result[:, a:b])
+            nc.scalar.copy(result[:, pairs], bank[:, 0, :])
+            nc.sync.dma_start(out[:, pairs], result[:, pairs])

import math
from contextlib import ExitStack

import concourse.mybir as mybir
from concourse.masks import make_identity

K, T, S, D, N, H, V, U = 1024, 4096, 1024, 4, 128, 512, 256, 512
FLOPS = 2 * K * H * S + 2 * H * N * U

F32 = mybir.dt.float32
BF16 = mybir.dt.bfloat16
I32 = mybir.dt.int32
U32 = mybir.dt.uint32
U16 = mybir.dt.uint16
U8 = mybir.dt.uint8
FP8X4 = mybir.dt.float8_e4m3fn_x4
ACT = mybir.ActivationFunctionType
ALU = mybir.AluOpType
AXIS = mybir.AxisListType

P = 128
PACK = 4
PASSES = K // (P * PACK)
QUADRANTS = 4
SCALE_ROWS = 4
LIST_ROWS = 16
HALVES = V // P
BLOCKS = H // P
RUN = P // PACK
GROUPS = 2
LOAD_BLOCKS = 2
KNEE = 32.0
BAG_WINDOW = 1024
TOP_WINDOW = 704
PAIR_CHUNK = 128
Y_BANKS = 4
TOP_ON_VECTOR = (U, U, U // 2, U // 2)


def tile_picked_ymilrk_top_p_kernel(
    tc, x_words, x_scales, hT, unit, w1, offs, pos, neg, out
):
    nc = tc.nc
    with ExitStack() as ctx:
        keep = ctx.enter_context(tc.tile_pool(name="keep", bufs=1))
        ring = ctx.enter_context(tc.tile_pool(name="ring", bufs=2))
        y_psum = ctx.enter_context(tc.psum_pool(name="y_psum", bufs=Y_BANKS))
        sum_psum = ctx.enter_context(tc.psum_pool(name="sum_psum", bufs=1))

        offs_t = keep.tile([P, S // LIST_ROWS], U16, name="offs_t")
        pos_t = keep.tile([P, U // LIST_ROWS], U16, name="pos_t")
        neg_t = keep.tile([P, U // LIST_ROWS], U16, name="neg_t")
        word_table = [keep.tile([P, T], U32, name=f"word_table{o}") for o in range(PASSES)]
        scale_table = keep.tile([P, T], U8, name="scale_table")
        h_raw = {}
        for first in range(0, BLOCKS, LOAD_BLOCKS):
            for o in range(PASSES):
                h_raw[first, o] = keep.tile([P, PACK, LOAD_BLOCKS * P], F32, name=f"h_raw{first}_{o}")
        unit_t = keep.tile([P, PACK], F32, name="unit_t")
        w_raw = keep.tile([P, PACK, N], F32, name="w_raw")

        def load_words(o, a, b):
            nc.sync.dma_start(
                word_table[o][:, a:b].bitcast(I32), x_words[o, :, a:b].rearrange("p n t -> p (n t)").bitcast(I32)
            )

        def load_scales(o):
            for q in range(QUADRANTS):
                row = 32 * q + SCALE_ROWS * o
                nc.sync.dma_start(
                    scale_table[row : row + SCALE_ROWS, :].bitcast(I32),
                    x_scales[o, SCALE_ROWS * q : SCALE_ROWS * (q + 1), :].bitcast(I32),
                )

        nc.vector.memset(scale_table[:].bitcast(I32), 0)
        load_words(0, 0, T // 2)
        load_scales(0)
        load_words(0, T // 2, T)
        nc.sync.dma_start(offs_t[:], offs)
        load_scales(1)
        load_words(1, 0, T)
        for first in range(0, BLOCKS, LOAD_BLOCKS):
            for o in range(PASSES):
                rows = hT[o * P * PACK : (o + 1) * P * PACK, first * P : (first + LOAD_BLOCKS) * P]
                nc.sync.dma_start(h_raw[first, o][:], rows.rearrange("(p j) n -> p j n", j=PACK))
        nc.sync.dma_start(unit_t[:], unit.rearrange("(p t) one -> p (t one)", t=PACK))
        nc.sync.dma_start(pos_t[:], pos)
        nc.sync.dma_start(neg_t[:], neg)
        nc.sync.dma_start(w_raw[:], w1.rearrange("(p j) m -> p j m", j=PACK))

        ident = keep.tile([P, P], F32, name="ident")
        make_identity(nc, ident[:])
        bag = [keep.tile([P, BAG_WINDOW], F32, name=f"bag{t}") for t in range(PACK)]
        top = [keep.tile([P, TOP_WINDOW], F32, name=f"top{t}") for t in range(PACK)]
        for t in range(PACK):
            nc.vector.memset(bag[t][:, V:], 0.0)
            nc.vector.memset(top[t][:, V:], 0.0)

        def from_rows(rows):
            return rows.rearrange("p j (c i) -> p c j i", i=2)

        def to_words(grouped):
            return grouped.rearrange("p (c i) j -> p c j i", i=2)

        scales_picked = keep.tile([P, S], U8, name="scales_picked")
        scales_dealt = keep.tile([P, HALVES, D, P], U8, name="scales_dealt", align_bytes=64)
        nc.vector.tensor_copy(scales_picked[:], scale_table[:].indirect(offs_t[:]))
        nc.vector.tensor_copy(scales_dealt[:], scales_picked[:].rearrange("p (h v d) -> p h d v", h=HALVES, d=D))
        words_dealt = {}
        list_cols = S // LIST_ROWS // HALVES
        for o in range(PASSES):
            for half in range(HALVES):
                words_dealt[o, half] = keep.tile([P, D, P], U32, name=f"words_dealt{o}_{half}", align_bytes=64)
                nc.vector.tensor_copy(
                    words_dealt[o, half][:].rearrange("p d v -> p v d"),
                    word_table[o][:].indirect(offs_t[:, half * list_cols : (half + 1) * list_cols]),
                )

        h_codes = {}
        h_scales = {}

        def quantize_h(c):
            first = c - c % LOAD_BLOCKS
            cols = slice((c - first) * P, (c - first + 1) * P)
            grouped = keep.tile([P, PASSES, P, PACK], BF16, name=f"h_grouped{c}", align_bytes=64)
            h_codes[c] = keep.tile([P, PASSES, P], U32, name=f"h_codes{c}", align_bytes=64)
            h_scales[c] = keep.tile([P, PASSES, P], U8, name=f"h_scales{c}", align_bytes=64)
            for o in range(PASSES):
                last_load = first + LOAD_BLOCKS == BLOCKS and o == PASSES - 1
                cast = nc.vector.tensor_copy if last_load else nc.scalar.copy
                cast(to_words(grouped[:, o]), from_rows(h_raw[first, o][:, :, cols]))
            nc.vector.quantize_mx(
                h_codes[c][:].rearrange("p o n -> p (o n)").bitcast(FP8X4),
                h_scales[c][:].rearrange("p o n -> p (o n)"),
                grouped[:].rearrange("p o n j -> p (o n j)"),
            )

        ww = [
            keep.tile([P, D, PACK, BLOCKS, RUN], F32, name=f"ww{half}", tag=f"ww{half}", align_bytes=64)
            for half in range(HALVES)
        ]
        wy = [keep.tile([P, D, PACK, BLOCKS, RUN], F32, name=f"wy{half}") for half in range(HALVES)]
        top_turned = [keep.tile([P, PACK, BLOCKS, RUN], F32, name=f"top_turned{half}") for half in range(HALVES)]

        def score(c, half):
            y = y_psum.tile([P, D, P], F32, name="bank")
            for d in range(D):
                for o in range(PASSES):
                    nc.tensor.matmul_mx(
                        y[:, d, :],
                        lhsT=words_dealt[o, half][:, d, :].bitcast(FP8X4),
                        lhsT_scale=scales_dealt[SCALE_ROWS * o :, half, d, :],
                        rhs=h_codes[c][:, o, :].bitcast(FP8X4),
                        rhs_scale=h_scales[c][:, o, :],
                        start=(o == 0),
                        stop=(o == PASSES - 1),
                    )
            y_by_slot = y[:].rearrange("p d (m t) -> p d t m", t=PACK)
            squashed = ring.tile([P, D, PACK, RUN], F32, name="squashed")
            nc.scalar.activation(squashed[:], y_by_slot, ACT.Tanh)
            nc.vector.tensor_reduce(
                top_turned[half][:, :, c, :], y[:].rearrange("p d (m t) -> p t m d", t=PACK), AXIS.X, ALU.max
            )
            nc.scalar.activation(ww[half][:, :, :, c, :], squashed[:], ACT.Exp, scale=1.5)
            nc.vector.tensor_tensor(wy[half][:, :, :, c, :], y_by_slot, ww[half][:, :, :, c, :], ALU.mult)

        for half in range(HALVES):
            for c in range(BLOCKS):
                if half == 0:
                    quantize_h(c)
                score(c, half)

        den = [sum_psum.tile([P, 2, HALVES, P], F32, name=f"den{g}") for g in range(GROUPS)]
        num = [sum_psum.tile([P, 2, HALVES, P], F32, name=f"num{g}") for g in range(GROUPS)]

        def turn_and_add(bank, members, half, g):
            for n in range(2):
                for d in range(D):
                    nc.tensor.matmul(
                        bank[:, n, half, :],
                        lhsT=members[:, d, 2 * g + n].rearrange("p c m -> p (c m)"),
                        rhs=ident[:],
                        is_transpose=True,
                        start=(d == 0),
                        stop=(d == D - 1),
                    )

        def turn_tops(g):
            bank = y_psum.tile([P, D, P], F32, name="bank")
            for n in range(2):
                for half in range(HALVES):
                    nc.tensor.transpose(
                        bank[:, 2 * n + half, :],
                        top_turned[half][:, 2 * g + n].rearrange("p c m -> p (c m)"),
                        ident[:],
                    )
            for n in range(2):
                t = 2 * g + n
                nc.vector.tensor_scalar_mul(
                    top[t][:, :V], bank[:, 2 * n : 2 * n + 2, :].rearrange("p h v -> p (h v)"), unit_t[:, t : t + 1]
                )

        for half in range(HALVES):
            for g in range(GROUPS):
                turn_and_add(den[g], ww[half], half, g)
        for g in range(GROUPS):
            turn_tops(g)
            for half in range(HALVES):
                turn_and_add(num[g], wy[half], half, g)

        log_den = keep.tile([P, GROUPS, 2 * V], F32, name="log_den", tag="log_den")
        inv_den = keep.tile([P, GROUPS, 2 * V], F32, name="inv_den")
        for g in range(GROUPS):
            nc.scalar.activation(log_den[:, g, :], den[g][:].rearrange("p n h v -> p (n h v)"), ACT.Ln)
        for n in range(2):
            cols = slice(n * V, (n + 1) * V)
            nc.scalar.activation(inv_den[:, :, cols], log_den[:, :, cols], ACT.Exp, scale=-1.0)
            for g in range(GROUPS):
                nc.vector.scalar_tensor_tensor(
                    bag[2 * g + n][:, :V],
                    num[g][:, n].rearrange("p h v -> p (h v)"),
                    1.0 / KNEE,
                    inv_den[:, g, cols],
                    ALU.mult,
                    ALU.mult,
                )
        slots_as_made = [2 * g + n for n in range(2) for g in range(GROUPS)]

        bag_pos = keep.tile([P, PACK, U], F32, name="bag_pos")
        gap = keep.tile([P, PACK, U], F32, name="gap")
        grown = keep.tile([P, PACK, U], F32, name="grown")
        for t in slots_as_made:
            nc.scalar.activation(bag_pos[:, t, :], bag[t][:].indirect(pos_t[:]), ACT.Copy)
        for t in slots_as_made:
            nc.vector.tensor_tensor(gap[:, t, :], bag[t][:].indirect(neg_t[:]), bag_pos[:, t, :], ALU.subtract)
            nc.scalar.activation(grown[:, t, :], gap[:, t, :], ACT.Exp, scale=KNEE)

        top_pos = {}
        for t in range(PACK):
            tag = "log_den" if t == PACK - 1 else f"top_pos{t}"
            top_pos[t] = keep.tile([P, U], F32, name="top_pos", tag=tag)
            cut = TOP_ON_VECTOR[t]
            nc.vector.tensor_copy(top_pos[t][:, :cut], top[t][:].indirect(pos_t[:, : cut // LIST_ROWS]))
            if cut < U:
                nc.scalar.activation(top_pos[t][:, cut:], top[t][:].indirect(pos_t[:, cut // LIST_ROWS :]), ACT.Copy)

        w_grouped = keep.tile([P, N, PACK], BF16, name="w_grouped", tag="ww0", align_bytes=64)
        w_codes = keep.tile([P, N], U32, name="w_codes", align_bytes=64)
        w_scales = keep.tile([P, N], U8, name="w_scales", align_bytes=64)
        nc.gpsimd.tensor_scalar(to_words(w_grouped[:]), from_rows(w_raw[:]), 1.0, 0.0, ALU.mult, ALU.add)
        nc.vector.quantize_mx(w_codes[:].bitcast(FP8X4), w_scales[:], w_grouped[:].rearrange("p m j -> p (m j)"))

        capped = keep.tile([P, PACK, U], F32, name="capped")
        factor = keep.tile([P, PACK, U], F32, name="factor")
        loss = keep.tile([P, PACK, U], F32, name="loss")
        hid = keep.tile([P, U, PACK], BF16, name="hid", align_bytes=64)
        hid_codes = keep.tile([P, U], U32, name="hid_codes", align_bytes=64)
        hid_scales = keep.tile([P, U], U8, name="hid_scales", align_bytes=64)
        result = keep.tile([P, U], F32, name="result")
        for slots in (slice(0, PACK - 1), slice(PACK - 1, PACK)):
            nc.vector.tensor_scalar_min(capped[:, slots, :], grown[:, slots, :], math.exp(KNEE))
        for t in range(PACK):
            nc.vector.scalar_tensor_tensor(factor[:, t, :], gap[:, t, :], 1.0, top_pos[t][:], ALU.max, ALU.mult)
        for a in range(0, U, PAIR_CHUNK):
            pairs = slice(a, a + PAIR_CHUNK)
            nc.scalar.activation(loss[:, :, pairs], capped[:, :, pairs], ACT.Ln, bias=1.0)
            nc.vector.tensor_tensor(
                to_words(hid[:, pairs, :]), from_rows(loss[:, :, pairs]), from_rows(factor[:, :, pairs]), ALU.mult
            )
            nc.vector.quantize_mx(
                hid_codes[:, pairs].bitcast(FP8X4), hid_scales[:, pairs], hid[:, pairs, :].rearrange("p r t -> p (r t)")
            )
            bank = y_psum.tile([P, D, P], F32, name="bank")
            nc.tensor.matmul_mx(
                bank[:, 0, :],
                lhsT=w_codes[:].bitcast(FP8X4),
                lhsT_scale=w_scales[:],
                rhs=hid_codes[:, pairs].bitcast(FP8X4),
                rhs_scale=hid_scales[:, pairs],
                start=True,
                stop=True,
            )
            nc.scalar.copy(result[:, pairs], bank[:, 0, :])
            nc.sync.dma_start(out[:, pairs], result[:, pairs])
